import numpy as np
import ml_dtypes


def mxq(x, axis, fmt="e4m3"):
    dtype, down = {"e4m3": (ml_dtypes.float8_e4m3fn, 7), "e5m2": (ml_dtypes.float8_e5m2, 14)}[fmt]
    v = np.moveaxis(np.asarray(x, np.float32).astype(ml_dtypes.bfloat16).astype(np.float64), axis, -1)
    blocks = v.reshape(v.shape[:-1] + (-1, 32))
    amax = np.abs(blocks).max(-1, keepdims=True)
    byte = np.maximum(np.where(amax > 0, np.frexp(amax)[1] - 1 + 127, 0) - down, 1)
    scale = np.exp2(byte - 127.0)
    codes = (blocks / scale).astype(np.float32).astype(dtype).astype(np.float64)
    return np.moveaxis((codes * scale).reshape(v.shape), -1, axis)


WIDE = False


def mx_kscale(k):
    if not WIDE:
        return np.ones(k)
    levels = np.array([10, -10, 5, -5, 0])
    if k % 512:
        return np.exp2(np.random.permutation(np.resize(levels, k // 32))).repeat(32)
    a = np.empty((k // 512, 16))
    for p in range(k // 512):
        a[p, :8] = np.random.permutation(np.resize(levels, 8))
        for g in range(8):
            far = levels[np.abs(levels - a[p, g]) >= 10]
            a[p, g + 8] = far[np.random.randint(len(far))]
    return np.exp2(a.ravel()).repeat(32)


def f64(x):
    return np.asarray(x).astype(np.float64)


def striped(idx):
    return np.tile(np.asarray(idx).reshape(-1, 16).T, (8, 1)).astype(np.uint16)


def unstriped(offs):
    return offs[:16].T.reshape(-1).astype(np.int64)


E2M1 = np.array([0.0, 0.5, 1.0, 1.5, 2.0, 3.0, 4.0, 6.0, -0.0, -0.5, -1.0, -1.5, -2.0, -3.0, -4.0, -6.0])


def pack_weight(w, fmt):
    k, n = w.shape
    w = f64(np.asarray(w, np.float32).astype(ml_dtypes.bfloat16)).reshape(k // 32, 32, n)
    amax = np.abs(w).max(1)
    if fmt == "e4m3":
        byte = np.frexp(amax)[1] - 1 + 127 - 7
    else:
        mant, ex = np.frexp(amax / 6.0)
        byte = np.where(mant > 0.5, ex, ex - 1) + 127
    byte = np.clip(np.where(amax > 0, byte, 1), 1, 254)
    scaled = (w * np.exp2(127.0 - byte)[:, None, :]).reshape(k, n).astype(np.float32)
    by_word = np.ascontiguousarray(scaled.reshape(k // 512, 128, 4, n).transpose(0, 1, 3, 2))
    if fmt == "e4m3":
        words = by_word.astype(ml_dtypes.float8_e4m3fn).view(np.uint8)
    else:
        c = by_word.astype(ml_dtypes.float4_e2m1fn).view(np.uint8) & 0xF
        words = (c[..., 0::2] | (c[..., 1::2] << 4)).reshape(k // 512, 128, 2 * n)
    return np.ascontiguousarray(words), np.ascontiguousarray(byte.astype(np.uint8).reshape(k // 512, 16, n))


def unpack_weight(words, scales, fmt):
    g, _, n = scales.shape
    words = np.ascontiguousarray(words).reshape(g, 128, n, -1)
    if fmt == "e4m3":
        vals = words.view(ml_dtypes.float8_e4m3fn).astype(np.float64)
    else:
        nib = np.empty((g, 128, n, 4), np.uint8)
        nib[..., 0::2] = words & 0xF
        nib[..., 1::2] = words >> 4
        vals = E2M1[nib]
    vals = vals * np.repeat(np.exp2(scales.astype(np.float64) - 127.0), 8, axis=1)[..., None]
    return vals.transpose(0, 1, 3, 2).reshape(g * 512, n)


def bf(x):
    return np.asarray(x, np.float32).astype(ml_dtypes.bfloat16)


def planes(Y):
    r, m = Y.shape
    b = f64(bf(Y)).reshape(r // 32, 32, m)
    amax = np.abs(b).max(1)
    byte = np.clip(np.where(amax > 0, np.frexp(amax)[1] - 1 + 127 - 7, 1), 1, 254)
    codes = (b * np.exp2(127.0 - byte)[:, None, :]).reshape(r, m).astype(np.float32).astype(ml_dtypes.float8_e4m3fn).view(np.uint8)
    words = codes.reshape(r // 512, 128, 4, m).transpose(0, 1, 3, 2)
    return np.ascontiguousarray(words), np.ascontiguousarray(byte.astype(np.uint8).reshape(r // 512, 16, m))


D, T, I, Q, E, K = 512, 2048, 512, 256, 512, 32


def setup_inputs():
    n = np.random.standard_normal
    idx = np.random.permutation(T)[:I]
    idx2 = np.random.permutation(T)[:I]
    idx3 = np.random.permutation(T)[:I]
    fd = mx_kscale(D)
    fi = mx_kscale(I)
    ti = np.ones(T)
    ti[idx] = fi
    keysp = pack_weight(n((D, T)) / fd[:, None], "e2m1")
    return {
        "query": (n((D, Q)) * 1.0 / np.sqrt(D) * fd[:, None]).astype(np.float32),
        "keys_words": keysp[0],
        "keys_scales": keysp[1],
        "lam": (np.random.uniform(0.4, 1.0, (Q, 1))).astype(np.float32),
        "os": (np.random.uniform(4.0, 16.0, (1, I)) * fi).astype(np.float32),
        "vals": (n((E, T)) / ti).astype(np.float32),
        "before": (n((E, Q))).astype(np.float32),
        "hold": (np.random.uniform(0.1, 0.6, (1, Q))).astype(np.float32),
        "offs": striped(idx),
        "offs2": striped(idx2),
        "offs3": striped(idx3),
    }


def reference(query, keys_words, keys_scales, lam, os, vals, before, hold, offs, offs2, offs3):
    idx = unstriped(offs)
    idx2 = unstriped(offs2)
    idx3 = unstriped(offs3)
    keysu = unpack_weight(keys_words, keys_scales, "e2m1")
    queryq = mxq(f64(query), 0, "e4m3")
    a = queryq.T @ keysu
    s = a[:, idx] + np.tanh(a[:, idx2] - a[:, idx3]) * f64(lam)
    p = np.exp(s - np.max(s, axis=1, keepdims=True))
    r = p / np.sum(p, axis=1, keepdims=True)
    rt = r.T
    rg = rt.reshape(I, K, Q // K).sum(axis=2)
    rq = 1.0 / np.sqrt(rg)
    rr = np.repeat(rq, Q // K, axis=1)
    w0 = rt * rr
    w = w0.T
    wo1 = w * f64(os)
    wt1 = wo1.T
    vt1 = f64(vals)[:, idx].T
    vt1q = mxq(vt1, 0, "e4m3")
    wt1q = mxq(wt1, 0, "e4m3")
    o = vt1q.T @ wt1q
    y = f64(before) * f64(hold) + o * (1.0 - f64(hold))
    words, scales = planes(y)
    return y, words, scales

@@ -1,0 +1,316 @@
+from contextlib import ExitStack
+
+import concourse.mybir as mybir
+from concourse.masks import make_identity
+
+D, T, I, Q, E, K = 512, 2048, 512, 256, 512, 32
+FLOPS = 2 * D * Q * T + 2 * I * E * Q
+
+F32 = mybir.dt.float32
+BF16 = mybir.dt.bfloat16
+I32 = mybir.dt.int32
+U32 = mybir.dt.uint32
+U16 = mybir.dt.uint16
+U8 = mybir.dt.uint8
+FP8X4 = mybir.dt.float8_e4m3fn_x4
+FP4X4 = mybir.dt.float4_e2m1fn_x4
+ACT = mybir.ActivationFunctionType
+ALU = mybir.AluOpType
+AXIS = mybir.AxisListType
+
+P = 128
+PACK = 4
+BANK = 512
+HALVES = Q // P
+GROUP = Q // K
+GROUPS = P // GROUP
+
+
+def tile_attend_seconded_balanced_blend_pl_kernel(
+    tc, query, keys_words, keys_scales, lam, slot_factor, vals, before, hold, offs, offs2, offs3, out_0, out_1, out_2
+):
+    nc = tc.nc
+    with ExitStack() as ctx:
+        keep = ctx.enter_context(tc.tile_pool(name="keep", bufs=1))
+        psum = ctx.enter_context(tc.psum_pool(name="psum", bufs=8))
+
+        def sbuf(name, shape, dtype, tag=None):
+            return keep.tile(shape, dtype, name=name, tag=tag or name, align_bytes=64)
+
+        def bank(shape):
+            return psum.tile(shape, F32, name="bank")
+
+        query_rows = query.rearrange("(p t) q -> p t q", t=PACK)
+        q_raw = [sbuf("q_raw%d" % h, [P, PACK, P], F32) for h in range(HALVES)]
+        key_words = [sbuf("key_words%d" % c, [P, T], U8) for c in range(2)]
+        key_scales = sbuf("key_scales", [P, T], U8)
+        own = sbuf("own", [P, I // 16], U16)
+        seconder = sbuf("seconder", [P, I // 16], U16)
+        opponent = sbuf("opponent", [P, I // 16], U16)
+        lam_col = sbuf("lam_col", [P, HALVES], F32)
+        hold_col = sbuf("hold_col", [P, HALVES], F32)
+        os_col = sbuf("os_col", [P, PACK], F32)
+        pool = [sbuf("pool%d" % j, [P, T], F32) for j in range(PACK)]
+        old = sbuf("old", [P, PACK, Q], F32)
+
+        nc.sync.dma_start(out=q_raw[0][:], in_=query_rows[:, :, 0:P])
+        for quad in range(4):
+            nc.sync.dma_start(
+                out=key_scales[32 * quad : 32 * quad + 4, :].bitcast(I32),
+                in_=keys_scales[0, 4 * quad : 4 * quad + 4, :].bitcast(I32),
+            )
+        for c in range(2):
+            nc.sync.dma_start(
+                out=key_words[c][:].bitcast(I32), in_=keys_words[0, :, c * T : (c + 1) * T].bitcast(I32)
+            )
+        nc.sync.dma_start(out=opponent[:], in_=offs3)
+        nc.sync.dma_start(out=seconder[:], in_=offs2)
+        nc.sync.dma_start(out=q_raw[1][:], in_=query_rows[:, :, P : 2 * P])
+        nc.sync.dma_start(out=own[:], in_=offs)
+        with nc.allow_non_contiguous_dma(reason="one value to a query row"):
+            nc.sync.dma_start(out=lam_col[:], in_=lam.rearrange("(h p) o -> p (h o)", p=P))
+        vals_rows = vals.rearrange("(p j) t -> j p t", j=PACK)
+        nc.sync.dma_start(out=old[:], in_=before.rearrange("(p j) q -> p j q", j=PACK))
+        with nc.allow_non_contiguous_dma(reason="one value to a query row"):
+            nc.sync.dma_start(out=hold_col[:], in_=hold.rearrange("o (h p) -> p (o h)", p=P))
+        nc.sync.dma_start(out=os_col[:], in_=slot_factor.rearrange("o (p t) -> p (o t)", t=PACK))
+        for j in range(PACK):
+            nc.sync.dma_start(out=pool[j][:], in_=vals_rows[j])
+
+        ident = sbuf("ident", [P, P], F32)
+        make_identity(nc, ident[:])
+        tiny = sbuf("tiny", [P, 1], F32)
+        nc.gpsimd.memset(tiny[:], 2.0**-100)
+
+        scores = []
+        for h in range(HALVES):
+            q_grouped = sbuf("q_grouped%d" % h, [P, P, PACK], BF16)
+            nc.vector.tensor_copy(out=q_grouped[:], in_=q_raw[h][:].rearrange("p t q -> p q t"))
+            q_codes = sbuf("q_codes%d" % h, [P, P], U32)
+            q_scales = sbuf("q_scales%d" % h, [P, P], U8)
+            nc.vector.quantize_mx(
+                out=q_codes[:].bitcast(FP8X4), scales=q_scales[:], in_=q_grouped[:].rearrange("p q t -> p (q t)")
+            )
+            a = sbuf("a%d" % h, [P, T], F32)
+            widths = [BANK, BANK, BANK, BANK // 2, BANK // 2] if h == 0 else [BANK] * 4
+            t0 = 0
+            for c, width in enumerate(widths):
+                acc = bank([P, width])
+                chunk, first = divmod(t0, T // 2)
+                nc.tensor.matmul_mx(
+                    out=acc[:],
+                    lhsT=q_codes[:].bitcast(FP8X4),
+                    lhsT_scale=q_scales[:],
+                    rhs=key_words[chunk][:, 2 * first : 2 * (first + width)].bitcast(FP4X4),
+                    rhs_scale=key_scales[:, t0 : t0 + width],
+                    start=True,
+                    stop=True,
+                )
+                if h == 0 and c % 2 == 0:
+                    nc.vector.tensor_copy(out=a[:, t0 : t0 + width], in_=acc[:])
+                else:
+                    nc.scalar.copy(out=a[:, t0 : t0 + width], in_=acc[:])
+                t0 += width
+            scores.append(a)
+
+        lean = []
+        for h in range(HALVES):
+            against = sbuf("against%d" % h, [P, I], F32)
+            nc.vector.tensor_copy(out=against[:], in_=scores[h][:].indirect(opponent[:]))
+            margin = sbuf("margin%d" % h, [P, I], F32)
+            nc.vector.tensor_tensor(
+                out=margin[:], in0=scores[h][:].indirect(seconder[:]), in1=against[:], op=ALU.subtract
+            )
+            bent = sbuf("bent%d" % h, [P, I], F32)
+            nc.scalar.activation(out=bent[:], in_=margin[:], func=ACT.Tanh)
+            u = sbuf("lean%d" % h, [P, I], F32)
+            nc.scalar.activation(out=u[:], in_=bent[:], func=ACT.Copy, scale=lam_col[:, h : h + 1])
+            lean.append(u)
+
+        v_codes = sbuf("v_codes", [P, E], U32)
+        v_scales = sbuf("v_scales", [P, E], U8)
+        v_grouped = [None] * PACK
+        shares_t = [None] * HALVES
+        weights = [None] * HALVES
+        inv_sum = [None] * HALVES
+        factor = [None] * HALVES
+        w_grouped = [None] * HALVES
+        w_quant = [None] * HALVES
+
+        def score_and_exp(h):
+            s = sbuf("s%d" % h, [P, I], F32)
+            nc.vector.tensor_tensor(out=s[:], in0=scores[h][:].indirect(own[:]), in1=lean[h][:], op=ALU.add)
+            neg_max = sbuf("neg_max%d" % h, [P, 1], F32)
+            nc.vector.tensor_reduce(out=neg_max[:], in_=s[:], axis=AXIS.X, op=ALU.max, negate=True)
+            p_dealt = sbuf("p_dealt%d" % h, [P, PACK, P], F32)
+            row_sum = sbuf("row_sum%d" % h, [P, 1], F32)
+            nc.scalar.activation(
+                out=p_dealt[:].rearrange("q t p -> q p t"),
+                in_=s[:].rearrange("q (p t) -> q p t", t=PACK),
+                func=ACT.Exp,
+                bias=neg_max[:],
+                scale=1.0,
+                accum_out=row_sum[:],
+            )
+            weights[h] = (p_dealt, row_sum)
+
+        def normalise(h):
+            p_dealt, row_sum = weights[h]
+            inv = sbuf("inv_sum%d" % h, [P, 1], F32, tag="pool0" if h == 1 else None)
+            nc.vector.reciprocal(out=inv[:], in_=row_sum[:])
+            r = sbuf("r%d" % h, [P, PACK, P], F32)
+            nc.vector.tensor_scalar(out=r[:], in0=p_dealt[:], scalar1=inv[:], scalar2=None, op0=ALU.mult)
+            rt = bank([P, PACK, P])
+            for t in range(PACK):
+                nc.tensor.transpose(rt[:, t, :], r[:, t, :], ident[:])
+            shares_t[h] = rt
+
+        def balance(h):
+            group_sum = sbuf("group_sum%d" % h, [P, GROUPS, PACK], F32, tag="pool%d" % (h + 1))
+            nc.vector.tensor_reduce(
+                out=group_sum[:].rearrange("p k t -> p t k"),
+                in_=shares_t[h][:].rearrange("p t (k j) -> p t k j", j=GROUP),
+                axis=AXIS.X,
+                op=ALU.add,
+            )
+            inv_root = sbuf("inv_root%d" % h, [P, GROUPS, PACK], F32, tag="s1" if h == 0 else None)
+            nc.scalar.activation(
+                out=inv_root[:], in_=group_sum[:], func=ACT.Abs_reciprocal_sqrt, bias=tiny[:], scale=1.0
+            )
+            factor[h] = inv_root
+
+        def weigh(h):
+            fac = factors[:, h]
+            nc.vector.tensor_tensor(
+                out=fac,
+                in0=factor[h][:],
+                in1=os_col[:].unsqueeze(1).to_broadcast([P, GROUPS, PACK]),
+                op=ALU.mult,
+            )
+            w_grouped[h] = sbuf("w_grouped%d" % h, [P, GROUPS, GROUP, PACK], BF16)
+            nc.vector.tensor_tensor(
+                out=w_grouped[h][:],
+                in0=shares_t[h][:].rearrange("p t (k j) -> p k j t", j=GROUP),
+                in1=fac.unsqueeze(2).to_broadcast([P, GROUPS, GROUP, PACK]),
+                op=ALU.mult,
+            )
+
+        def quantise_weights(h):
+            w_codes = sbuf("w_codes%d" % h, [P, P], U32)
+            w_scales = sbuf("w_scales%d" % h, [P, P], U8)
+            nc.vector.quantize_mx(
+                out=w_codes[:].bitcast(FP8X4),
+                scales=w_scales[:],
+                in_=w_grouped[h][:].rearrange("p k j t -> p (k j t)"),
+            )
+            w_quant[h] = (w_codes, w_scales)
+
+        def pick_values(j, tag):
+            picked = sbuf("picked%d" % j, [P, I], BF16, tag=tag)
+            nc.vector.tensor_copy(out=picked[:], in_=pool[j][:].indirect(own[:]))
+            pairs = picked[:].bitcast(F32)
+            turned = bank([P, 2, P])
+            for u in range(2):
+                nc.tensor.transpose(turned[:, u, :], pairs[:, u : I // 2 : 2], ident[:])
+            v_grouped[j] = sbuf("v_grouped%d" % j, [P, P * PACK], BF16)
+            nc.scalar.copy(
+                out=v_grouped[j][:].bitcast(F32).rearrange("p (e u) -> p e u", u=2),
+                in_=turned[:].rearrange("p u e -> p e u"),
+            )
+
+        def quantise_values(j):
+            nc.vector.quantize_mx(
+                out=v_codes[:, j * P : (j + 1) * P].bitcast(FP8X4),
+                scales=v_scales[:, j * P : (j + 1) * P],
+                in_=v_grouped[j][:],
+            )
+
+        score_and_exp(0)
+        score_and_exp(1)
+        normalise(0)
+        pick_values(0, "lean1")
+        normalise(1)
+        pick_values(1, "p_dealt0")
+        balance(0)
+
+        let_go = sbuf("let_go", [P, HALVES], F32)
+        nc.gpsimd.tensor_scalar(
+            out=let_go[:], in0=hold_col[:], scalar1=-1.0, scalar2=1.0, op0=ALU.mult, op1=ALU.add
+        )
+        pick_values(2, "p_dealt1")
+        balance(1)
+        pick_values(3, None)
+
+        y_banks = []
+        for h in range(HALVES):
+            old_t = bank([P, PACK, P])
+            for j in range(PACK):
+                nc.tensor.transpose(old_t[:, j, :], old[:, j, h * P : (h + 1) * P], ident[:])
+            kept_t = sbuf("kept_t%d" % h, [P, PACK, P], F32)
+            nc.scalar.activation(out=kept_t[:], in_=old_t[:], func=ACT.Copy, scale=hold_col[:, h : h + 1])
+            y_bank = bank([P, PACK, P])
+            for j in range(PACK):
+                nc.tensor.matmul(
+                    y_bank[:, j, :], kept_t[:, j, :], ident[:], start=(j == 0), stop=False, is_transpose=True
+                )
+            y_banks.append(y_bank)
+
+        factors = sbuf("factors", [P, HALVES, GROUPS, PACK], F32, tag="pool3")
+        weigh(0)
+        for j in range(PACK - 1):
+            quantise_values(j)
+        quantise_weights(0)
+        quantise_values(PACK - 1)
+        weigh(1)
+        quantise_weights(1)
+
+        y_codes = sbuf("y_codes", [P, Q], U32)
+        y_scales = sbuf("y_scales", [P, Q], U8)
+        out_rows = out_0.rearrange("(p j) q -> p j q", j=PACK)
+        out_words = out_1[0].rearrange("p c r -> p (c r)").bitcast(I32)
+        news = []
+        for h in range(HALVES):
+            w_codes, w_scales = w_quant[h]
+            o_t = bank([P, PACK, P])
+            nc.tensor.matmul_mx(
+                out=o_t[:].rearrange("q j p -> q (j p)"),
+                lhsT=w_codes[:].bitcast(FP8X4),
+                lhsT_scale=w_scales[:],
+                rhs=v_codes[:].bitcast(FP8X4),
+                rhs_scale=v_scales[:],
+                start=True,
+                stop=True,
+            )
+            new_t = sbuf("new_t%d" % h, [P, PACK, P], F32)
+            if h == 0:
+                nc.scalar.activation(out=new_t[:], in_=o_t[:], func=ACT.Copy, scale=let_go[:, h : h + 1])
+            else:
+                nc.vector.tensor_scalar(
+                    out=new_t[:], in0=o_t[:], scalar1=let_go[:, h : h + 1], scalar2=None, op0=ALU.mult
+                )
+            news.append(new_t)
+        for h in range(HALVES):
+            y_bank = y_banks[h]
+            for j in range(PACK):
+                nc.tensor.matmul(
+                    y_bank[:, j, :], news[h][:, j, :], ident[:], start=False, stop=(j == PACK - 1), is_transpose=True
+                )
+            y = sbuf("y%d" % h, [P, PACK, P], F32)
+            nc.scalar.copy(out=y[:], in_=y_bank[:])
+            nc.sync.dma_start(out=out_rows[:, :, h * P : (h + 1) * P], in_=y[:])
+            y_grouped = sbuf("y_grouped%d" % h, [P, P, PACK], BF16)
+            nc.vector.tensor_copy(out=y_grouped[:], in_=y[:].rearrange("p j q -> p q j"))
+            nc.vector.quantize_mx(
+                out=y_codes[:, h * P : (h + 1) * P].bitcast(FP8X4),
+                scales=y_scales[:, h * P : (h + 1) * P],
+                in_=y_grouped[:].rearrange("p q j -> p (q j)"),
+            )
+            nc.sync.dma_start(
+                out=out_words[:, h * P : (h + 1) * P], in_=y_codes[:, h * P : (h + 1) * P].bitcast(I32)
+            )
+        for quad in range(4):
+            queue = nc.scalar if quad % 2 else nc.sync
+            queue.dma_start(
+                out=out_2[0, 4 * quad : 4 * quad + 4, :].bitcast(I32),
+                in_=y_scales[32 * quad : 32 * quad + 4, :].bitcast(I32),
+            )

@@ -70,11 +70,12 @@ def tile_attend_seconded_balanced_blend_pl_kernel(
         with nc.allow_non_contiguous_dma(reason="one value to a query row"):
             nc.sync.dma_start(out=lam_col[:], in_=lam.rearrange("(h p) o -> p (h o)", p=P))
         vals_rows = vals.rearrange("(p j) t -> j p t", j=PACK)
-        nc.sync.dma_start(out=old[:], in_=before.rearrange("(p j) q -> p j q", j=PACK))
+        nc.sync.dma_start(out=pool[0][:], in_=vals_rows[0])
         with nc.allow_non_contiguous_dma(reason="one value to a query row"):
             nc.sync.dma_start(out=hold_col[:], in_=hold.rearrange("o (h p) -> p (o h)", p=P))
+        nc.sync.dma_start(out=old[:], in_=before.rearrange("(p j) q -> p j q", j=PACK))
         nc.sync.dma_start(out=os_col[:], in_=slot_factor.rearrange("o (p t) -> p (o t)", t=PACK))
-        for j in range(PACK):
+        for j in range(1, PACK):
             nc.sync.dma_start(out=pool[j][:], in_=vals_rows[j])
 
         ident = sbuf("ident", [P, P], F32)
@@ -114,6 +115,7 @@ def tile_attend_seconded_balanced_blend_pl_kernel(
             scores.append(a)
 
         lean = []
+        kept = []
         for h in range(HALVES):
             against = sbuf("against%d" % h, [P, I], F32)
             nc.vector.tensor_copy(out=against[:], in_=scores[h][:].indirect(opponent[:]))
@@ -126,14 +128,21 @@ def tile_attend_seconded_balanced_blend_pl_kernel(
             u = sbuf("lean%d" % h, [P, I], F32)
             nc.scalar.activation(out=u[:], in_=bent[:], func=ACT.Copy, scale=lam_col[:, h : h + 1])
             lean.append(u)
+            old_t = bank([P, PACK, P])
+            for j in range(PACK):
+                nc.tensor.transpose(old_t[:, j, :], old[:, j, h * P : (h + 1) * P], ident[:])
+            kept_t = sbuf("kept_t%d" % h, [P, PACK, P], F32)
+            nc.scalar.activation(out=kept_t[:], in_=old_t[:], func=ACT.Copy, scale=hold_col[:, h : h + 1])
+            kept_bank = bank([P, PACK, P])
+            for j in range(PACK):
+                nc.tensor.transpose(kept_bank[:, j, :], kept_t[:, j, :], ident[:])
+            kept.append(kept_bank)
 
         v_codes = sbuf("v_codes", [P, E], U32)
         v_scales = sbuf("v_scales", [P, E], U8)
         v_grouped = [None] * PACK
         shares_t = [None] * HALVES
         weights = [None] * HALVES
-        inv_sum = [None] * HALVES
-        factor = [None] * HALVES
         w_grouped = [None] * HALVES
         w_quant = [None] * HALVES
 
@@ -156,42 +165,21 @@ def tile_attend_seconded_balanced_blend_pl_kernel(
 
         def normalise(h):
             p_dealt, row_sum = weights[h]
-            inv = sbuf("inv_sum%d" % h, [P, 1], F32, tag="pool0" if h == 1 else None)
+            inv = sbuf("inv_sum%d" % h, [P, 1], F32)
             nc.vector.reciprocal(out=inv[:], in_=row_sum[:])
             r = sbuf("r%d" % h, [P, PACK, P], F32)
-            nc.vector.tensor_scalar(out=r[:], in0=p_dealt[:], scalar1=inv[:], scalar2=None, op0=ALU.mult)
+            nc.scalar.activation(out=r[:], in_=p_dealt[:], func=ACT.Copy, scale=inv[:])
             rt = bank([P, PACK, P])
             for t in range(PACK):
                 nc.tensor.transpose(rt[:, t, :], r[:, t, :], ident[:])
             shares_t[h] = rt
 
-        def balance(h):
-            group_sum = sbuf("group_sum%d" % h, [P, GROUPS, PACK], F32, tag="pool%d" % (h + 1))
-            nc.vector.tensor_reduce(
-                out=group_sum[:].rearrange("p k t -> p t k"),
-                in_=shares_t[h][:].rearrange("p t (k j) -> p t k j", j=GROUP),
-                axis=AXIS.X,
-                op=ALU.add,
-            )
-            inv_root = sbuf("inv_root%d" % h, [P, GROUPS, PACK], F32, tag="s1" if h == 0 else None)
-            nc.scalar.activation(
-                out=inv_root[:], in_=group_sum[:], func=ACT.Abs_reciprocal_sqrt, bias=tiny[:], scale=1.0
-            )
-            factor[h] = inv_root
-
         def weigh(h):
-            fac = factors[:, h]
-            nc.vector.tensor_tensor(
-                out=fac,
-                in0=factor[h][:],
-                in1=os_col[:].unsqueeze(1).to_broadcast([P, GROUPS, PACK]),
-                op=ALU.mult,
-            )
             w_grouped[h] = sbuf("w_grouped%d" % h, [P, GROUPS, GROUP, PACK], BF16)
             nc.vector.tensor_tensor(
                 out=w_grouped[h][:],
                 in0=shares_t[h][:].rearrange("p t (k j) -> p k j t", j=GROUP),
-                in1=fac.unsqueeze(2).to_broadcast([P, GROUPS, GROUP, PACK]),
+                in1=factor[:, h * GROUPS : (h + 1) * GROUPS, :].unsqueeze(2).to_broadcast([P, GROUPS, GROUP, PACK]),
                 op=ALU.mult,
             )
 
@@ -208,11 +196,14 @@ def tile_attend_seconded_balanced_blend_pl_kernel(
         def pick_values(j, tag):
             picked = sbuf("picked%d" % j, [P, I], BF16, tag=tag)
             nc.vector.tensor_copy(out=picked[:], in_=pool[j][:].indirect(own[:]))
+            turn_values(j, picked, None)
+
+        def turn_values(j, picked, grouped_tag):
             pairs = picked[:].bitcast(F32)
             turned = bank([P, 2, P])
             for u in range(2):
                 nc.tensor.transpose(turned[:, u, :], pairs[:, u : I // 2 : 2], ident[:])
-            v_grouped[j] = sbuf("v_grouped%d" % j, [P, P * PACK], BF16)
+            v_grouped[j] = sbuf("v_grouped%d" % j, [P, P * PACK], BF16, tag=grouped_tag)
             nc.scalar.copy(
                 out=v_grouped[j][:].bitcast(F32).rearrange("p (e u) -> p e u", u=2),
                 in_=turned[:].rearrange("p u e -> p e u"),
@@ -230,32 +221,33 @@ def tile_attend_seconded_balanced_blend_pl_kernel(
         normalise(0)
         pick_values(0, "lean1")
         normalise(1)
-        pick_values(1, "p_dealt0")
-        balance(0)
-
-        let_go = sbuf("let_go", [P, HALVES], F32)
-        nc.gpsimd.tensor_scalar(
-            out=let_go[:], in0=hold_col[:], scalar1=-1.0, scalar2=1.0, op0=ALU.mult, op1=ALU.add
-        )
-        pick_values(2, "p_dealt1")
-        balance(1)
-        pick_values(3, None)
-
-        y_banks = []
+        hold_rows = bank([P, HALVES, P])
         for h in range(HALVES):
-            old_t = bank([P, PACK, P])
-            for j in range(PACK):
-                nc.tensor.transpose(old_t[:, j, :], old[:, j, h * P : (h + 1) * P], ident[:])
-            kept_t = sbuf("kept_t%d" % h, [P, PACK, P], F32)
-            nc.scalar.activation(out=kept_t[:], in_=old_t[:], func=ACT.Copy, scale=hold_col[:, h : h + 1])
-            y_bank = bank([P, PACK, P])
-            for j in range(PACK):
-                nc.tensor.matmul(
-                    y_bank[:, j, :], kept_t[:, j, :], ident[:], start=(j == 0), stop=False, is_transpose=True
-                )
-            y_banks.append(y_bank)
+            nc.tensor.transpose(hold_rows[:, h, :], hold_col[:, h : h + 1].to_broadcast([P, P]), ident[:])
+        let_go = sbuf("let_go", [P, HALVES, P], F32)
+        nc.scalar.activation(out=let_go[:], in_=hold_rows[:], func=ACT.Copy, scale=-1.0, bias=1.0)
+        pick_values(1, "row_sum1")
 
-        factors = sbuf("factors", [P, HALVES, GROUPS, PACK], F32, tag="pool3")
+        picked2 = sbuf("picked2", [P, I], BF16, tag="s1")
+        nc.vector.tensor_copy(out=picked2[:], in_=pool[2][:].indirect(own[:]))
+        group_sum = sbuf("group_sum", [P, K, PACK], F32, tag="pool2")
+        for h in range(HALVES):
+            nc.vector.tensor_reduce(
+                out=group_sum[:, h * GROUPS : (h + 1) * GROUPS, :].rearrange("p k t -> p t k"),
+                in_=shares_t[h][:].rearrange("p t (k j) -> p t k j", j=GROUP),
+                axis=AXIS.X,
+                op=ALU.add,
+            )
+        inv_root = sbuf("inv_root", [P, K, PACK], F32)
+        nc.scalar.activation(
+            out=inv_root[:], in_=group_sum[:], func=ACT.Abs_reciprocal_sqrt, bias=tiny[:], scale=1.0
+        )
+        turn_values(2, picked2, "pool2")
+        pick_values(3, "s0")
+        factor = sbuf("factor", [P, K, PACK], F32, tag="pool3")
+        nc.vector.tensor_tensor(
+            out=factor[:], in0=inv_root[:], in1=os_col[:].unsqueeze(1).to_broadcast([P, K, PACK]), op=ALU.mult
+        )
         weigh(0)
         for j in range(PACK - 1):
             quantise_values(j)
@@ -268,46 +260,40 @@ def tile_attend_seconded_balanced_blend_pl_kernel(
         y_scales = sbuf("y_scales", [P, Q], U8)
         out_rows = out_0.rearrange("(p j) q -> p j q", j=PACK)
         out_words = out_1[0].rearrange("p c r -> p (c r)").bitcast(I32)
-        news = []
+        y_grouped = []
         for h in range(HALVES):
             w_codes, w_scales = w_quant[h]
-            o_t = bank([P, PACK, P])
-            nc.tensor.matmul_mx(
-                out=o_t[:].rearrange("q j p -> q (j p)"),
-                lhsT=w_codes[:].bitcast(FP8X4),
-                lhsT_scale=w_scales[:],
-                rhs=v_codes[:].bitcast(FP8X4),
-                rhs_scale=v_scales[:],
-                start=True,
-                stop=True,
-            )
-            new_t = sbuf("new_t%d" % h, [P, PACK, P], F32)
-            if h == 0:
-                nc.scalar.activation(out=new_t[:], in_=o_t[:], func=ACT.Copy, scale=let_go[:, h : h + 1])
-            else:
-                nc.vector.tensor_scalar(
-                    out=new_t[:], in0=o_t[:], scalar1=let_go[:, h : h + 1], scalar2=None, op0=ALU.mult
-                )
-            news.append(new_t)
-        for h in range(HALVES):
-            y_bank = y_banks[h]
+            o = bank([P, PACK, P])
             for j in range(PACK):
-                nc.tensor.matmul(
-                    y_bank[:, j, :], news[h][:, j, :], ident[:], start=False, stop=(j == PACK - 1), is_transpose=True
+                nc.tensor.matmul_mx(
+                    out=o[:, j, :],
+                    lhsT=v_codes[:, j * P : (j + 1) * P].bitcast(FP8X4),
+                    lhsT_scale=v_scales[:, j * P : (j + 1) * P],
+                    rhs=w_codes[:].bitcast(FP8X4),
+                    rhs_scale=w_scales[:],
+                    start=True,
+                    stop=True,
                 )
+            fresh = sbuf("fresh%d" % h, [P, PACK, P], F32)
+            nc.vector.tensor_tensor(
+                out=fresh[:], in0=o[:], in1=let_go[:, h : h + 1, :].to_broadcast([P, PACK, P]), op=ALU.mult
+            )
             y = sbuf("y%d" % h, [P, PACK, P], F32)
-            nc.scalar.copy(out=y[:], in_=y_bank[:])
+            nc.vector.tensor_tensor(out=y[:], in0=kept[h][:], in1=fresh[:], op=ALU.add)
             nc.sync.dma_start(out=out_rows[:, :, h * P : (h + 1) * P], in_=y[:])
-            y_grouped = sbuf("y_grouped%d" % h, [P, P, PACK], BF16)
-            nc.vector.tensor_copy(out=y_grouped[:], in_=y[:].rearrange("p j q -> p q j"))
+            grouped = sbuf("y_grouped%d" % h, [P, P, PACK], BF16)
+            if h == 0:
+                nc.scalar.copy(out=grouped[:], in_=y[:].rearrange("p j q -> p q j"))
+            else:
+                nc.vector.tensor_copy(out=grouped[:], in_=y[:].rearrange("p j q -> p q j"))
+            y_grouped.append(grouped)
+        for h in range(HALVES):
             nc.vector.quantize_mx(
                 out=y_codes[:, h * P : (h + 1) * P].bitcast(FP8X4),
                 scales=y_scales[:, h * P : (h + 1) * P],
-                in_=y_grouped[:].rearrange("p q j -> p (q j)"),
+                in_=y_grouped[h][:].rearrange("p q j -> p (q j)"),
             )
-            nc.sync.dma_start(
-                out=out_words[:, h * P : (h + 1) * P], in_=y_codes[:, h * P : (h + 1) * P].bitcast(I32)
-            )
+        nc.scalar.dma_start(out=out_words, in_=y_codes[:].bitcast(I32))
         for quad in range(4):
             queue = nc.scalar if quad % 2 else nc.sync
             queue.dma_start(

@@ -42,7 +42,7 @@ def tile_attend_seconded_balanced_blend_pl_kernel(
 
         query_rows = query.rearrange("(p t) q -> p t q", t=PACK)
         q_raw = [sbuf("q_raw%d" % h, [P, PACK, P], F32) for h in range(HALVES)]
-        key_words = [sbuf("key_words%d" % c, [P, T], U8) for c in range(2)]
+        key_words = [sbuf("key_words%d" % c, [P, 2 * BANK], U8) for c in range(T // BANK)]
         key_scales = sbuf("key_scales", [P, T], U8)
         own = sbuf("own", [P, I // 16], U16)
         seconder = sbuf("seconder", [P, I // 16], U16)
@@ -59,13 +59,14 @@ def tile_attend_seconded_balanced_blend_pl_kernel(
                 out=key_scales[32 * quad : 32 * quad + 4, :].bitcast(I32),
                 in_=keys_scales[0, 4 * quad : 4 * quad + 4, :].bitcast(I32),
             )
-        for c in range(2):
+        for c in range(T // BANK):
             nc.sync.dma_start(
-                out=key_words[c][:].bitcast(I32), in_=keys_words[0, :, c * T : (c + 1) * T].bitcast(I32)
+                out=key_words[c][:].bitcast(I32),
+                in_=keys_words[0, :, c * 2 * BANK : (c + 1) * 2 * BANK].bitcast(I32),
             )
+        nc.sync.dma_start(out=q_raw[1][:], in_=query_rows[:, :, P : 2 * P])
         nc.sync.dma_start(out=opponent[:], in_=offs3)
         nc.sync.dma_start(out=seconder[:], in_=offs2)
-        nc.sync.dma_start(out=q_raw[1][:], in_=query_rows[:, :, P : 2 * P])
         nc.sync.dma_start(out=own[:], in_=offs)
         with nc.allow_non_contiguous_dma(reason="one value to a query row"):
             nc.sync.dma_start(out=lam_col[:], in_=lam.rearrange("(h p) o -> p (h o)", p=P))
@@ -97,7 +98,7 @@ def tile_attend_seconded_balanced_blend_pl_kernel(
             t0 = 0
             for c, width in enumerate(widths):
                 acc = bank([P, width])
-                chunk, first = divmod(t0, T // 2)
+                chunk, first = divmod(t0, BANK)
                 nc.tensor.matmul_mx(
                     out=acc[:],
                     lhsT=q_codes[:].bitcast(FP8X4),
@@ -117,13 +118,13 @@ def tile_attend_seconded_balanced_blend_pl_kernel(
         lean = []
         kept = []
         for h in range(HALVES):
-            against = sbuf("against%d" % h, [P, I], F32)
+            against = sbuf("against%d" % h, [P, I], F32, tag="q_grouped1" if h == 0 else None)
             nc.vector.tensor_copy(out=against[:], in_=scores[h][:].indirect(opponent[:]))
             margin = sbuf("margin%d" % h, [P, I], F32)
             nc.vector.tensor_tensor(
                 out=margin[:], in0=scores[h][:].indirect(seconder[:]), in1=against[:], op=ALU.subtract
             )
-            bent = sbuf("bent%d" % h, [P, I], F32)
+            bent = sbuf("bent%d" % h, [P, I], F32, tag="key_words3" if h == 0 else None)
             nc.scalar.activation(out=bent[:], in_=margin[:], func=ACT.Tanh)
             u = sbuf("lean%d" % h, [P, I], F32)
             nc.scalar.activation(out=u[:], in_=bent[:], func=ACT.Copy, scale=lam_col[:, h : h + 1])
@@ -147,15 +148,15 @@ def tile_attend_seconded_balanced_blend_pl_kernel(
         w_quant = [None] * HALVES
 
         def score_and_exp(h):
-            s = sbuf("s%d" % h, [P, I], F32)
+            s = sbuf("s%d" % h, [P, I], F32, tag="against1" if h == 0 else None)
             nc.vector.tensor_tensor(out=s[:], in0=scores[h][:].indirect(own[:]), in1=lean[h][:], op=ALU.add)
             neg_max = sbuf("neg_max%d" % h, [P, 1], F32)
             nc.vector.tensor_reduce(out=neg_max[:], in_=s[:], axis=AXIS.X, op=ALU.max, negate=True)
-            p_dealt = sbuf("p_dealt%d" % h, [P, PACK, P], F32)
+            p_dealt = sbuf("p_dealt%d" % h, [P, I], F32, tag="kept_t%d" % h)
             row_sum = sbuf("row_sum%d" % h, [P, 1], F32)
             nc.scalar.activation(
-                out=p_dealt[:].rearrange("q t p -> q p t"),
-                in_=s[:].rearrange("q (p t) -> q p t", t=PACK),
+                out=p_dealt[:],
+                in_=s[:],
                 func=ACT.Exp,
                 bias=neg_max[:],
                 scale=1.0,
@@ -167,12 +168,28 @@ def tile_attend_seconded_balanced_blend_pl_kernel(
             p_dealt, row_sum = weights[h]
             inv = sbuf("inv_sum%d" % h, [P, 1], F32)
             nc.vector.reciprocal(out=inv[:], in_=row_sum[:])
-            r = sbuf("r%d" % h, [P, PACK, P], F32)
+            r = sbuf("r%d" % h, [P, I], F32)
             nc.scalar.activation(out=r[:], in_=p_dealt[:], func=ACT.Copy, scale=inv[:])
             rt = bank([P, PACK, P])
             for t in range(PACK):
-                nc.tensor.transpose(rt[:, t, :], r[:, t, :], ident[:])
+                nc.tensor.transpose(rt[:, t, :], r[:, t:I:PACK], ident[:])
             shares_t[h] = rt
+
+        def balance(h):
+            group_sum = sbuf("group_sum%d" % h, [P, GROUPS, PACK], F32, tag="pool%d" % (h + 1))
+            nc.vector.tensor_reduce(
+                out=group_sum[:],
+                in_=shares_t[h][:].rearrange("p t (k j) -> p k t j", j=GROUP),
+                axis=AXIS.X,
+                op=ALU.add,
+            )
+            nc.scalar.activation(
+                out=inv_root[:, h * GROUPS : (h + 1) * GROUPS, :],
+                in_=group_sum[:],
+                func=ACT.Abs_reciprocal_sqrt,
+                bias=tiny[:],
+                scale=1.0,
+            )
 
         def weigh(h):
             w_grouped[h] = sbuf("w_grouped%d" % h, [P, GROUPS, GROUP, PACK], BF16)
@@ -196,14 +213,11 @@ def tile_attend_seconded_balanced_blend_pl_kernel(
         def pick_values(j, tag):
             picked = sbuf("picked%d" % j, [P, I], BF16, tag=tag)
             nc.vector.tensor_copy(out=picked[:], in_=pool[j][:].indirect(own[:]))
-            turn_values(j, picked, None)
-
-        def turn_values(j, picked, grouped_tag):
             pairs = picked[:].bitcast(F32)
             turned = bank([P, 2, P])
             for u in range(2):
                 nc.tensor.transpose(turned[:, u, :], pairs[:, u : I // 2 : 2], ident[:])
-            v_grouped[j] = sbuf("v_grouped%d" % j, [P, P * PACK], BF16, tag=grouped_tag)
+            v_grouped[j] = sbuf("v_grouped%d" % j, [P, P * PACK], BF16)
             nc.scalar.copy(
                 out=v_grouped[j][:].bitcast(F32).rearrange("p (e u) -> p e u", u=2),
                 in_=turned[:].rearrange("p u e -> p e u"),
@@ -219,31 +233,20 @@ def tile_attend_seconded_balanced_blend_pl_kernel(
         score_and_exp(0)
         score_and_exp(1)
         normalise(0)
-        pick_values(0, "lean1")
+        pick_values(0, "against1")
         normalise(1)
         hold_rows = bank([P, HALVES, P])
         for h in range(HALVES):
             nc.tensor.transpose(hold_rows[:, h, :], hold_col[:, h : h + 1].to_broadcast([P, P]), ident[:])
         let_go = sbuf("let_go", [P, HALVES, P], F32)
         nc.scalar.activation(out=let_go[:], in_=hold_rows[:], func=ACT.Copy, scale=-1.0, bias=1.0)
-        pick_values(1, "row_sum1")
+        pick_values(1, "s1")
 
-        picked2 = sbuf("picked2", [P, I], BF16, tag="s1")
-        nc.vector.tensor_copy(out=picked2[:], in_=pool[2][:].indirect(own[:]))
-        group_sum = sbuf("group_sum", [P, K, PACK], F32, tag="pool2")
-        for h in range(HALVES):
-            nc.vector.tensor_reduce(
-                out=group_sum[:, h * GROUPS : (h + 1) * GROUPS, :].rearrange("p k t -> p t k"),
-                in_=shares_t[h][:].rearrange("p t (k j) -> p t k j", j=GROUP),
-                axis=AXIS.X,
-                op=ALU.add,
-            )
         inv_root = sbuf("inv_root", [P, K, PACK], F32)
-        nc.scalar.activation(
-            out=inv_root[:], in_=group_sum[:], func=ACT.Abs_reciprocal_sqrt, bias=tiny[:], scale=1.0
-        )
-        turn_values(2, picked2, "pool2")
-        pick_values(3, "s0")
+        balance(0)
+        pick_values(2, None)
+        balance(1)
+        pick_values(3, None)
         factor = sbuf("factor", [P, K, PACK], F32, tag="pool3")
         nc.vector.tensor_tensor(
             out=factor[:], in0=inv_root[:], in1=os_col[:].unsqueeze(1).to_broadcast([P, K, PACK]), op=ALU.mult
@@ -293,9 +296,10 @@ def tile_attend_seconded_balanced_blend_pl_kernel(
                 scales=y_scales[:, h * P : (h + 1) * P],
                 in_=y_grouped[h][:].rearrange("p q j -> p (q j)"),
             )
-        nc.scalar.dma_start(out=out_words, in_=y_codes[:].bitcast(I32))
+            queue = nc.sync if h else nc.scalar
+            queue.dma_start(out=out_words[:, h * P : (h + 1) * P], in_=y_codes[:, h * P : (h + 1) * P].bitcast(I32))
         for quad in range(4):
-            queue = nc.scalar if quad % 2 else nc.sync
+            queue = nc.sync if quad % 2 else nc.scalar
             queue.dma_start(
                 out=out_2[0, 4 * quad : 4 * quad + 4, :].bitcast(I32),
                 in_=y_scales[32 * quad : 32 * quad + 4, :].bitcast(I32),

@@ -64,7 +64,8 @@ def tile_attend_seconded_balanced_blend_pl_kernel(
                 out=key_words[c][:].bitcast(I32),
                 in_=keys_words[0, :, c * 2 * BANK : (c + 1) * 2 * BANK].bitcast(I32),
             )
-        nc.sync.dma_start(out=q_raw[1][:], in_=query_rows[:, :, P : 2 * P])
+            if c == 1:
+                nc.sync.dma_start(out=q_raw[1][:], in_=query_rows[:, :, P : 2 * P])
         nc.sync.dma_start(out=opponent[:], in_=offs3)
         nc.sync.dma_start(out=seconder[:], in_=offs2)
         nc.sync.dma_start(out=own[:], in_=offs)
@@ -87,7 +88,10 @@ def tile_attend_seconded_balanced_blend_pl_kernel(
         scores = []
         for h in range(HALVES):
             q_grouped = sbuf("q_grouped%d" % h, [P, P, PACK], BF16)
-            nc.vector.tensor_copy(out=q_grouped[:], in_=q_raw[h][:].rearrange("p t q -> p q t"))
+            nc.vector.tensor_copy(
+                out=q_grouped[:].rearrange("p (c i) t -> p c t i", i=PACK),
+                in_=q_raw[h][:].rearrange("p t (c i) -> p c t i", i=PACK),
+            )
             q_codes = sbuf("q_codes%d" % h, [P, P], U32)
             q_scales = sbuf("q_scales%d" % h, [P, P], U8)
             nc.vector.quantize_mx(
@@ -108,7 +112,7 @@ def tile_attend_seconded_balanced_blend_pl_kernel(
                     start=True,
                     stop=True,
                 )
-                if h == 0 and c % 2 == 0:
+                if h == 0 and c in (2, 4):
                     nc.vector.tensor_copy(out=a[:, t0 : t0 + width], in_=acc[:])
                 else:
                     nc.scalar.copy(out=a[:, t0 : t0 + width], in_=acc[:])
@@ -145,6 +149,7 @@ def tile_attend_seconded_balanced_blend_pl_kernel(
         shares_t = [None] * HALVES
         weights = [None] * HALVES
         w_grouped = [None] * HALVES
+        inv_root = [None] * HALVES
         w_quant = [None] * HALVES
 
         def score_and_exp(h):
@@ -176,15 +181,16 @@ def tile_attend_seconded_balanced_blend_pl_kernel(
             shares_t[h] = rt
 
         def balance(h):
-            group_sum = sbuf("group_sum%d" % h, [P, GROUPS, PACK], F32, tag="pool%d" % (h + 1))
+            group_sum = sbuf("group_sum%d" % h, [P, GROUPS, PACK], F32, tag="pool3" if h == 1 else None)
             nc.vector.tensor_reduce(
                 out=group_sum[:],
                 in_=shares_t[h][:].rearrange("p t (k j) -> p k t j", j=GROUP),
                 axis=AXIS.X,
                 op=ALU.add,
             )
+            inv_root[h] = sbuf("inv_root%d" % h, [P, GROUPS, PACK], F32)
             nc.scalar.activation(
-                out=inv_root[:, h * GROUPS : (h + 1) * GROUPS, :],
+                out=inv_root[h][:],
                 in_=group_sum[:],
                 func=ACT.Abs_reciprocal_sqrt,
                 bias=tiny[:],
@@ -192,11 +198,18 @@ def tile_attend_seconded_balanced_blend_pl_kernel(
             )
 
         def weigh(h):
+            factor = sbuf("factor%d" % h, [P, GROUPS, PACK], F32)
+            nc.vector.tensor_tensor(
+                out=factor[:],
+                in0=inv_root[h][:],
+                in1=os_col[:].unsqueeze(1).to_broadcast([P, GROUPS, PACK]),
+                op=ALU.mult,
+            )
             w_grouped[h] = sbuf("w_grouped%d" % h, [P, GROUPS, GROUP, PACK], BF16)
             nc.vector.tensor_tensor(
                 out=w_grouped[h][:],
                 in0=shares_t[h][:].rearrange("p t (k j) -> p k j t", j=GROUP),
-                in1=factor[:, h * GROUPS : (h + 1) * GROUPS, :].unsqueeze(2).to_broadcast([P, GROUPS, GROUP, PACK]),
+                in1=factor[:].unsqueeze(2).to_broadcast([P, GROUPS, GROUP, PACK]),
                 op=ALU.mult,
             )
 
@@ -242,15 +255,10 @@ def tile_attend_seconded_balanced_blend_pl_kernel(
         nc.scalar.activation(out=let_go[:], in_=hold_rows[:], func=ACT.Copy, scale=-1.0, bias=1.0)
         pick_values(1, "s1")
 
-        inv_root = sbuf("inv_root", [P, K, PACK], F32)
         balance(0)
         pick_values(2, None)
-        balance(1)
         pick_values(3, None)
-        factor = sbuf("factor", [P, K, PACK], F32, tag="pool3")
-        nc.vector.tensor_tensor(
-            out=factor[:], in0=inv_root[:], in1=os_col[:].unsqueeze(1).to_broadcast([P, K, PACK]), op=ALU.mult
-        )
+        balance(1)
         weigh(0)
         for j in range(PACK - 1):
             quantise_values(j)
@@ -285,10 +293,12 @@ def tile_attend_seconded_balanced_blend_pl_kernel(
             nc.vector.tensor_tensor(out=y[:], in0=kept[h][:], in1=fresh[:], op=ALU.add)
             nc.sync.dma_start(out=out_rows[:, :, h * P : (h + 1) * P], in_=y[:])
             grouped = sbuf("y_grouped%d" % h, [P, P, PACK], BF16)
+            grouped_view = grouped[:].rearrange("p (c i) j -> p c j i", i=PACK)
+            y_view = y[:].rearrange("p j (c i) -> p c j i", i=PACK)
             if h == 0:
-                nc.scalar.copy(out=grouped[:], in_=y[:].rearrange("p j q -> p q j"))
+                nc.scalar.copy(out=grouped_view, in_=y_view)
             else:
-                nc.vector.tensor_copy(out=grouped[:], in_=y[:].rearrange("p j q -> p q j"))
+                nc.vector.tensor_copy(out=grouped_view, in_=y_view)
             y_grouped.append(grouped)
         for h in range(HALVES):
             nc.vector.quantize_mx(

@@ -21,9 +21,13 @@ AXIS = mybir.AxisListType
 P = 128
 PACK = 4
 BANK = 512
+PSUM_BANKS = 8
 HALVES = Q // P
 GROUP = Q // K
 GROUPS = P // GROUP
+QUADRANTS = 4
+LIST_COLUMNS = I // 16
+KEY_WORD_BYTES = 2
 
 
 def tile_attend_seconded_balanced_blend_pl_kernel(
@@ -32,7 +36,7 @@ def tile_attend_seconded_balanced_blend_pl_kernel(
     nc = tc.nc
     with ExitStack() as ctx:
         keep = ctx.enter_context(tc.tile_pool(name="keep", bufs=1))
-        psum = ctx.enter_context(tc.psum_pool(name="psum", bufs=8))
+        psum = ctx.enter_context(tc.psum_pool(name="psum", bufs=PSUM_BANKS))
 
         def sbuf(name, shape, dtype, tag=None):
             return keep.tile(shape, dtype, name=name, tag=tag or name, align_bytes=64)
@@ -42,11 +46,11 @@ def tile_attend_seconded_balanced_blend_pl_kernel(
 
         query_rows = query.rearrange("(p t) q -> p t q", t=PACK)
         q_raw = [sbuf("q_raw%d" % h, [P, PACK, P], F32) for h in range(HALVES)]
-        key_words = [sbuf("key_words%d" % c, [P, 2 * BANK], U8) for c in range(T // BANK)]
+        key_words = [sbuf("key_words%d" % c, [P, KEY_WORD_BYTES * BANK], U8) for c in range(T // BANK)]
         key_scales = sbuf("key_scales", [P, T], U8)
-        own = sbuf("own", [P, I // 16], U16)
-        seconder = sbuf("seconder", [P, I // 16], U16)
-        opponent = sbuf("opponent", [P, I // 16], U16)
+        own = sbuf("own", [P, LIST_COLUMNS], U16)
+        seconder = sbuf("seconder", [P, LIST_COLUMNS], U16)
+        opponent = sbuf("opponent", [P, LIST_COLUMNS], U16)
         lam_col = sbuf("lam_col", [P, HALVES], F32)
         hold_col = sbuf("hold_col", [P, HALVES], F32)
         os_col = sbuf("os_col", [P, PACK], F32)
@@ -54,17 +58,15 @@ def tile_attend_seconded_balanced_blend_pl_kernel(
         old = sbuf("old", [P, PACK, Q], F32)
 
         nc.sync.dma_start(out=q_raw[0][:], in_=query_rows[:, :, 0:P])
-        for quad in range(4):
+        for quad in range(QUADRANTS):
             nc.sync.dma_start(
                 out=key_scales[32 * quad : 32 * quad + 4, :].bitcast(I32),
                 in_=keys_scales[0, 4 * quad : 4 * quad + 4, :].bitcast(I32),
             )
         for c in range(T // BANK):
-            nc.sync.dma_start(
-                out=key_words[c][:].bitcast(I32),
-                in_=keys_words[0, :, c * 2 * BANK : (c + 1) * 2 * BANK].bitcast(I32),
-            )
-            if c == 1:
+            piece_bytes = slice(c * KEY_WORD_BYTES * BANK, (c + 1) * KEY_WORD_BYTES * BANK)
+            nc.sync.dma_start(out=key_words[c][:].bitcast(I32), in_=keys_words[0, :, piece_bytes].bitcast(I32))
+            if c == T // BANK // 2 - 1:
                 nc.sync.dma_start(out=q_raw[1][:], in_=query_rows[:, :, P : 2 * P])
         nc.sync.dma_start(out=opponent[:], in_=offs3)
         nc.sync.dma_start(out=seconder[:], in_=offs2)
@@ -98,21 +100,22 @@ def tile_attend_seconded_balanced_blend_pl_kernel(
                 out=q_codes[:].bitcast(FP8X4), scales=q_scales[:], in_=q_grouped[:].rearrange("p q t -> p (q t)")
             )
             a = sbuf("a%d" % h, [P, T], F32)
-            widths = [BANK, BANK, BANK, BANK // 2, BANK // 2] if h == 0 else [BANK] * 4
+            widths = [BANK, BANK, BANK, BANK // 2, BANK // 2] if h == 0 else [BANK] * (T // BANK)
+            on_vector = (2, 4) if h == 0 else ()
             t0 = 0
             for c, width in enumerate(widths):
                 acc = bank([P, width])
-                chunk, first = divmod(t0, BANK)
+                piece, first = divmod(t0, BANK)
                 nc.tensor.matmul_mx(
                     out=acc[:],
                     lhsT=q_codes[:].bitcast(FP8X4),
                     lhsT_scale=q_scales[:],
-                    rhs=key_words[chunk][:, 2 * first : 2 * (first + width)].bitcast(FP4X4),
+                    rhs=key_words[piece][:, KEY_WORD_BYTES * first : KEY_WORD_BYTES * (first + width)].bitcast(FP4X4),
                     rhs_scale=key_scales[:, t0 : t0 + width],
                     start=True,
                     stop=True,
                 )
-                if h == 0 and c in (2, 4):
+                if c in on_vector:
                     nc.vector.tensor_copy(out=a[:, t0 : t0 + width], in_=acc[:])
                 else:
                     nc.scalar.copy(out=a[:, t0 : t0 + width], in_=acc[:])
@@ -128,11 +131,12 @@ def tile_attend_seconded_balanced_blend_pl_kernel(
             nc.vector.tensor_tensor(
                 out=margin[:], in0=scores[h][:].indirect(seconder[:]), in1=against[:], op=ALU.subtract
             )
-            bent = sbuf("bent%d" % h, [P, I], F32, tag="key_words3" if h == 0 else None)
+            bent = sbuf("bent%d" % h, [P, I], F32, tag="key_words3" if h == 0 else "kept_t0")
             nc.scalar.activation(out=bent[:], in_=margin[:], func=ACT.Tanh)
-            u = sbuf("lean%d" % h, [P, I], F32)
-            nc.scalar.activation(out=u[:], in_=bent[:], func=ACT.Copy, scale=lam_col[:, h : h + 1])
-            lean.append(u)
+            lean_h = sbuf("lean%d" % h, [P, I], F32)
+            nc.scalar.activation(out=lean_h[:], in_=bent[:], func=ACT.Copy, scale=lam_col[:, h : h + 1])
+            lean.append(lean_h)
+
             old_t = bank([P, PACK, P])
             for j in range(PACK):
                 nc.tensor.transpose(old_t[:, j, :], old[:, j, h * P : (h + 1) * P], ident[:])
@@ -146,10 +150,10 @@ def tile_attend_seconded_balanced_blend_pl_kernel(
         v_codes = sbuf("v_codes", [P, E], U32)
         v_scales = sbuf("v_scales", [P, E], U8)
         v_grouped = [None] * PACK
+        exps = [None] * HALVES
         shares_t = [None] * HALVES
-        weights = [None] * HALVES
-        w_grouped = [None] * HALVES
         inv_root = [None] * HALVES
+        w_grouped = [None] * HALVES
         w_quant = [None] * HALVES
 
         def score_and_exp(h):
@@ -157,44 +161,34 @@ def tile_attend_seconded_balanced_blend_pl_kernel(
             nc.vector.tensor_tensor(out=s[:], in0=scores[h][:].indirect(own[:]), in1=lean[h][:], op=ALU.add)
             neg_max = sbuf("neg_max%d" % h, [P, 1], F32)
             nc.vector.tensor_reduce(out=neg_max[:], in_=s[:], axis=AXIS.X, op=ALU.max, negate=True)
-            p_dealt = sbuf("p_dealt%d" % h, [P, I], F32, tag="kept_t%d" % h)
+            raised = sbuf("raised%d" % h, [P, I], F32, tag="kept_t%d" % h)
             row_sum = sbuf("row_sum%d" % h, [P, 1], F32)
             nc.scalar.activation(
-                out=p_dealt[:],
-                in_=s[:],
-                func=ACT.Exp,
-                bias=neg_max[:],
-                scale=1.0,
-                accum_out=row_sum[:],
+                out=raised[:], in_=s[:], func=ACT.Exp, bias=neg_max[:], scale=1.0, accum_out=row_sum[:]
             )
-            weights[h] = (p_dealt, row_sum)
+            exps[h] = (raised, row_sum)
 
         def normalise(h):
-            p_dealt, row_sum = weights[h]
-            inv = sbuf("inv_sum%d" % h, [P, 1], F32)
-            nc.vector.reciprocal(out=inv[:], in_=row_sum[:])
+            raised, row_sum = exps[h]
+            inv_sum = sbuf("inv_sum%d" % h, [P, 1], F32)
+            nc.vector.reciprocal(out=inv_sum[:], in_=row_sum[:])
             r = sbuf("r%d" % h, [P, I], F32)
-            nc.scalar.activation(out=r[:], in_=p_dealt[:], func=ACT.Copy, scale=inv[:])
-            rt = bank([P, PACK, P])
+            nc.scalar.activation(out=r[:], in_=raised[:], func=ACT.Copy, scale=inv_sum[:])
+            shares_t[h] = bank([P, PACK, P])
             for t in range(PACK):
-                nc.tensor.transpose(rt[:, t, :], r[:, t:I:PACK], ident[:])
-            shares_t[h] = rt
+                nc.tensor.transpose(shares_t[h][:, t, :], r[:, t:I:PACK], ident[:])
 
         def balance(h):
             group_sum = sbuf("group_sum%d" % h, [P, GROUPS, PACK], F32, tag="pool3" if h == 1 else None)
             nc.vector.tensor_reduce(
                 out=group_sum[:],
-                in_=shares_t[h][:].rearrange("p t (k j) -> p k t j", j=GROUP),
+                in_=shares_t[h][:].rearrange("p t (k g) -> p k t g", g=GROUP),
                 axis=AXIS.X,
                 op=ALU.add,
             )
             inv_root[h] = sbuf("inv_root%d" % h, [P, GROUPS, PACK], F32)
             nc.scalar.activation(
-                out=inv_root[h][:],
-                in_=group_sum[:],
-                func=ACT.Abs_reciprocal_sqrt,
-                bias=tiny[:],
-                scale=1.0,
+                out=inv_root[h][:], in_=group_sum[:], func=ACT.Abs_reciprocal_sqrt, bias=tiny[:], scale=1.0
             )
 
         def weigh(h):
@@ -208,7 +202,7 @@ def tile_attend_seconded_balanced_blend_pl_kernel(
             w_grouped[h] = sbuf("w_grouped%d" % h, [P, GROUPS, GROUP, PACK], BF16)
             nc.vector.tensor_tensor(
                 out=w_grouped[h][:],
-                in0=shares_t[h][:].rearrange("p t (k j) -> p k j t", j=GROUP),
+                in0=shares_t[h][:].rearrange("p t (k g) -> p k g t", g=GROUP),
                 in1=factor[:].unsqueeze(2).to_broadcast([P, GROUPS, GROUP, PACK]),
                 op=ALU.mult,
             )
@@ -219,11 +213,11 @@ def tile_attend_seconded_balanced_blend_pl_kernel(
             nc.vector.quantize_mx(
                 out=w_codes[:].bitcast(FP8X4),
                 scales=w_scales[:],
-                in_=w_grouped[h][:].rearrange("p k j t -> p (k j t)"),
+                in_=w_grouped[h][:].rearrange("p k g t -> p (k g t)"),
             )
             w_quant[h] = (w_codes, w_scales)
 
-        def pick_values(j, tag):
+        def pick_values(j, tag=None):
             picked = sbuf("picked%d" % j, [P, I], BF16, tag=tag)
             nc.vector.tensor_copy(out=picked[:], in_=pool[j][:].indirect(own[:]))
             pairs = picked[:].bitcast(F32)
@@ -246,18 +240,17 @@ def tile_attend_seconded_balanced_blend_pl_kernel(
         score_and_exp(0)
         score_and_exp(1)
         normalise(0)
-        pick_values(0, "against1")
+        pick_values(0, tag="against1")
         normalise(1)
         hold_rows = bank([P, HALVES, P])
         for h in range(HALVES):
             nc.tensor.transpose(hold_rows[:, h, :], hold_col[:, h : h + 1].to_broadcast([P, P]), ident[:])
         let_go = sbuf("let_go", [P, HALVES, P], F32)
         nc.scalar.activation(out=let_go[:], in_=hold_rows[:], func=ACT.Copy, scale=-1.0, bias=1.0)
-        pick_values(1, "s1")
-
+        pick_values(1, tag="s1")
         balance(0)
-        pick_values(2, None)
-        pick_values(3, None)
+        pick_values(2)
+        pick_values(3)
         balance(1)
         weigh(0)
         for j in range(PACK - 1):
@@ -306,9 +299,9 @@ def tile_attend_seconded_balanced_blend_pl_kernel(
                 scales=y_scales[:, h * P : (h + 1) * P],
                 in_=y_grouped[h][:].rearrange("p q j -> p (q j)"),
             )
-            queue = nc.sync if h else nc.scalar
+            queue = nc.sync if h % 2 else nc.scalar
             queue.dma_start(out=out_words[:, h * P : (h + 1) * P], in_=y_codes[:, h * P : (h + 1) * P].bitcast(I32))
-        for quad in range(4):
+        for quad in range(QUADRANTS):
             queue = nc.sync if quad % 2 else nc.scalar
             queue.dma_start(
                 out=out_2[0, 4 * quad : 4 * quad + 4, :].bitcast(I32),

from contextlib import ExitStack

import concourse.mybir as mybir
from concourse.masks import make_identity

D, T, I, Q, E, K = 512, 2048, 512, 256, 512, 32
FLOPS = 2 * D * Q * T + 2 * I * E * Q

F32 = mybir.dt.float32
BF16 = mybir.dt.bfloat16
I32 = mybir.dt.int32
U32 = mybir.dt.uint32
U16 = mybir.dt.uint16
U8 = mybir.dt.uint8
FP8X4 = mybir.dt.float8_e4m3fn_x4
FP4X4 = mybir.dt.float4_e2m1fn_x4
ACT = mybir.ActivationFunctionType
ALU = mybir.AluOpType
AXIS = mybir.AxisListType

P = 128
PACK = 4
BANK = 512
PSUM_BANKS = 8
HALVES = Q // P
GROUP = Q // K
GROUPS = P // GROUP
QUADRANTS = 4
LIST_COLUMNS = I // 16
KEY_WORD_BYTES = 2


def tile_attend_seconded_balanced_blend_pl_kernel(
    tc, query, keys_words, keys_scales, lam, slot_factor, vals, before, hold, offs, offs2, offs3, out_0, out_1, out_2
):
    nc = tc.nc
    with ExitStack() as ctx:
        keep = ctx.enter_context(tc.tile_pool(name="keep", bufs=1))
        psum = ctx.enter_context(tc.psum_pool(name="psum", bufs=PSUM_BANKS))

        def sbuf(name, shape, dtype, tag=None):
            return keep.tile(shape, dtype, name=name, tag=tag or name, align_bytes=64)

        def bank(shape):
            return psum.tile(shape, F32, name="bank")

        query_rows = query.rearrange("(p t) q -> p t q", t=PACK)
        q_raw = [sbuf("q_raw%d" % h, [P, PACK, P], F32) for h in range(HALVES)]
        key_words = [sbuf("key_words%d" % c, [P, KEY_WORD_BYTES * BANK], U8) for c in range(T // BANK)]
        key_scales = sbuf("key_scales", [P, T], U8)
        own = sbuf("own", [P, LIST_COLUMNS], U16)
        seconder = sbuf("seconder", [P, LIST_COLUMNS], U16)
        opponent = sbuf("opponent", [P, LIST_COLUMNS], U16)
        lam_col = sbuf("lam_col", [P, HALVES], F32)
        hold_col = sbuf("hold_col", [P, HALVES], F32)
        os_col = sbuf("os_col", [P, PACK], F32)
        pool = [sbuf("pool%d" % j, [P, T], F32) for j in range(PACK)]
        old = sbuf("old", [P, PACK, Q], F32)

        nc.sync.dma_start(out=q_raw[0][:], in_=query_rows[:, :, 0:P])
        for quad in range(QUADRANTS):
            nc.sync.dma_start(
                out=key_scales[32 * quad : 32 * quad + 4, :].bitcast(I32),
                in_=keys_scales[0, 4 * quad : 4 * quad + 4, :].bitcast(I32),
            )
        for c in range(T // BANK):
            piece_bytes = slice(c * KEY_WORD_BYTES * BANK, (c + 1) * KEY_WORD_BYTES * BANK)
            nc.sync.dma_start(out=key_words[c][:].bitcast(I32), in_=keys_words[0, :, piece_bytes].bitcast(I32))
            if c == T // BANK // 2 - 1:
                nc.sync.dma_start(out=q_raw[1][:], in_=query_rows[:, :, P : 2 * P])
        nc.sync.dma_start(out=opponent[:], in_=offs3)
        nc.sync.dma_start(out=seconder[:], in_=offs2)
        nc.sync.dma_start(out=own[:], in_=offs)
        with nc.allow_non_contiguous_dma(reason="one value to a query row"):
            nc.sync.dma_start(out=lam_col[:], in_=lam.rearrange("(h p) o -> p (h o)", p=P))
        vals_rows = vals.rearrange("(p j) t -> j p t", j=PACK)
        nc.sync.dma_start(out=pool[0][:], in_=vals_rows[0])
        with nc.allow_non_contiguous_dma(reason="one value to a query row"):
            nc.sync.dma_start(out=hold_col[:], in_=hold.rearrange("o (h p) -> p (o h)", p=P))
        nc.sync.dma_start(out=old[:], in_=before.rearrange("(p j) q -> p j q", j=PACK))
        nc.sync.dma_start(out=os_col[:], in_=slot_factor.rearrange("o (p t) -> p (o t)", t=PACK))
        for j in range(1, PACK):
            nc.sync.dma_start(out=pool[j][:], in_=vals_rows[j])

        ident = sbuf("ident", [P, P], F32)
        make_identity(nc, ident[:])
        tiny = sbuf("tiny", [P, 1], F32)
        nc.gpsimd.memset(tiny[:], 2.0**-100)

        scores = []
        for h in range(HALVES):
            q_grouped = sbuf("q_grouped%d" % h, [P, P, PACK], BF16)
            nc.vector.tensor_copy(
                out=q_grouped[:].rearrange("p (c i) t -> p c t i", i=PACK),
                in_=q_raw[h][:].rearrange("p t (c i) -> p c t i", i=PACK),
            )
            q_codes = sbuf("q_codes%d" % h, [P, P], U32)
            q_scales = sbuf("q_scales%d" % h, [P, P], U8)
            nc.vector.quantize_mx(
                out=q_codes[:].bitcast(FP8X4), scales=q_scales[:], in_=q_grouped[:].rearrange("p q t -> p (q t)")
            )
            a = sbuf("a%d" % h, [P, T], F32)
            widths = [BANK, BANK, BANK, BANK // 2, BANK // 2] if h == 0 else [BANK] * (T // BANK)
            on_vector = (2, 4) if h == 0 else ()
            t0 = 0
            for c, width in enumerate(widths):
                acc = bank([P, width])
                piece, first = divmod(t0, BANK)
                nc.tensor.matmul_mx(
                    out=acc[:],
                    lhsT=q_codes[:].bitcast(FP8X4),
                    lhsT_scale=q_scales[:],
                    rhs=key_words[piece][:, KEY_WORD_BYTES * first : KEY_WORD_BYTES * (first + width)].bitcast(FP4X4),
                    rhs_scale=key_scales[:, t0 : t0 + width],
                    start=True,
                    stop=True,
                )
                if c in on_vector:
                    nc.vector.tensor_copy(out=a[:, t0 : t0 + width], in_=acc[:])
                else:
                    nc.scalar.copy(out=a[:, t0 : t0 + width], in_=acc[:])
                t0 += width
            scores.append(a)

        lean = []
        kept = []
        for h in range(HALVES):
            against = sbuf("against%d" % h, [P, I], F32, tag="q_grouped1" if h == 0 else None)
            nc.vector.tensor_copy(out=against[:], in_=scores[h][:].indirect(opponent[:]))
            margin = sbuf("margin%d" % h, [P, I], F32)
            nc.vector.tensor_tensor(
                out=margin[:], in0=scores[h][:].indirect(seconder[:]), in1=against[:], op=ALU.subtract
            )
            bent = sbuf("bent%d" % h, [P, I], F32, tag="key_words3" if h == 0 else "kept_t0")
            nc.scalar.activation(out=bent[:], in_=margin[:], func=ACT.Tanh)
            lean_h = sbuf("lean%d" % h, [P, I], F32)
            nc.scalar.activation(out=lean_h[:], in_=bent[:], func=ACT.Copy, scale=lam_col[:, h : h + 1])
            lean.append(lean_h)

            old_t = bank([P, PACK, P])
            for j in range(PACK):
                nc.tensor.transpose(old_t[:, j, :], old[:, j, h * P : (h + 1) * P], ident[:])
            kept_t = sbuf("kept_t%d" % h, [P, PACK, P], F32)
            nc.scalar.activation(out=kept_t[:], in_=old_t[:], func=ACT.Copy, scale=hold_col[:, h : h + 1])
            kept_bank = bank([P, PACK, P])
            for j in range(PACK):
                nc.tensor.transpose(kept_bank[:, j, :], kept_t[:, j, :], ident[:])
            kept.append(kept_bank)

        v_codes = sbuf("v_codes", [P, E], U32)
        v_scales = sbuf("v_scales", [P, E], U8)
        v_grouped = [None] * PACK
        exps = [None] * HALVES
        shares_t = [None] * HALVES
        inv_root = [None] * HALVES
        w_grouped = [None] * HALVES
        w_quant = [None] * HALVES

        def score_and_exp(h):
            s = sbuf("s%d" % h, [P, I], F32, tag="against1" if h == 0 else None)
            nc.vector.tensor_tensor(out=s[:], in0=scores[h][:].indirect(own[:]), in1=lean[h][:], op=ALU.add)
            neg_max = sbuf("neg_max%d" % h, [P, 1], F32)
            nc.vector.tensor_reduce(out=neg_max[:], in_=s[:], axis=AXIS.X, op=ALU.max, negate=True)
            raised = sbuf("raised%d" % h, [P, I], F32, tag="kept_t%d" % h)
            row_sum = sbuf("row_sum%d" % h, [P, 1], F32)
            nc.scalar.activation(
                out=raised[:], in_=s[:], func=ACT.Exp, bias=neg_max[:], scale=1.0, accum_out=row_sum[:]
            )
            exps[h] = (raised, row_sum)

        def normalise(h):
            raised, row_sum = exps[h]
            inv_sum = sbuf("inv_sum%d" % h, [P, 1], F32)
            nc.vector.reciprocal(out=inv_sum[:], in_=row_sum[:])
            r = sbuf("r%d" % h, [P, I], F32)
            nc.scalar.activation(out=r[:], in_=raised[:], func=ACT.Copy, scale=inv_sum[:])
            shares_t[h] = bank([P, PACK, P])
            for t in range(PACK):
                nc.tensor.transpose(shares_t[h][:, t, :], r[:, t:I:PACK], ident[:])

        def balance(h):
            group_sum = sbuf("group_sum%d" % h, [P, GROUPS, PACK], F32, tag="pool3" if h == 1 else None)
            nc.vector.tensor_reduce(
                out=group_sum[:],
                in_=shares_t[h][:].rearrange("p t (k g) -> p k t g", g=GROUP),
                axis=AXIS.X,
                op=ALU.add,
            )
            inv_root[h] = sbuf("inv_root%d" % h, [P, GROUPS, PACK], F32)
            nc.scalar.activation(
                out=inv_root[h][:], in_=group_sum[:], func=ACT.Abs_reciprocal_sqrt, bias=tiny[:], scale=1.0
            )

        def weigh(h):
            factor = sbuf("factor%d" % h, [P, GROUPS, PACK], F32)
            nc.vector.tensor_tensor(
                out=factor[:],
                in0=inv_root[h][:],
                in1=os_col[:].unsqueeze(1).to_broadcast([P, GROUPS, PACK]),
                op=ALU.mult,
            )
            w_grouped[h] = sbuf("w_grouped%d" % h, [P, GROUPS, GROUP, PACK], BF16)
            nc.vector.tensor_tensor(
                out=w_grouped[h][:],
                in0=shares_t[h][:].rearrange("p t (k g) -> p k g t", g=GROUP),
                in1=factor[:].unsqueeze(2).to_broadcast([P, GROUPS, GROUP, PACK]),
                op=ALU.mult,
            )

        def quantise_weights(h):
            w_codes = sbuf("w_codes%d" % h, [P, P], U32)
            w_scales = sbuf("w_scales%d" % h, [P, P], U8)
            nc.vector.quantize_mx(
                out=w_codes[:].bitcast(FP8X4),
                scales=w_scales[:],
                in_=w_grouped[h][:].rearrange("p k g t -> p (k g t)"),
            )
            w_quant[h] = (w_codes, w_scales)

        def pick_values(j, tag=None):
            picked = sbuf("picked%d" % j, [P, I], BF16, tag=tag)
            nc.vector.tensor_copy(out=picked[:], in_=pool[j][:].indirect(own[:]))
            pairs = picked[:].bitcast(F32)
            turned = bank([P, 2, P])
            for u in range(2):
                nc.tensor.transpose(turned[:, u, :], pairs[:, u : I // 2 : 2], ident[:])
            v_grouped[j] = sbuf("v_grouped%d" % j, [P, P * PACK], BF16)
            nc.scalar.copy(
                out=v_grouped[j][:].bitcast(F32).rearrange("p (e u) -> p e u", u=2),
                in_=turned[:].rearrange("p u e -> p e u"),
            )

        def quantise_values(j):
            nc.vector.quantize_mx(
                out=v_codes[:, j * P : (j + 1) * P].bitcast(FP8X4),
                scales=v_scales[:, j * P : (j + 1) * P],
                in_=v_grouped[j][:],
            )

        score_and_exp(0)
        score_and_exp(1)
        normalise(0)
        pick_values(0, tag="against1")
        normalise(1)
        hold_rows = bank([P, HALVES, P])
        for h in range(HALVES):
            nc.tensor.transpose(hold_rows[:, h, :], hold_col[:, h : h + 1].to_broadcast([P, P]), ident[:])
        let_go = sbuf("let_go", [P, HALVES, P], F32)
        nc.scalar.activation(out=let_go[:], in_=hold_rows[:], func=ACT.Copy, scale=-1.0, bias=1.0)
        pick_values(1, tag="s1")
        balance(0)
        pick_values(2)
        pick_values(3)
        balance(1)
        weigh(0)
        for j in range(PACK - 1):
            quantise_values(j)
        quantise_weights(0)
        quantise_values(PACK - 1)
        weigh(1)
        quantise_weights(1)

        y_codes = sbuf("y_codes", [P, Q], U32)
        y_scales = sbuf("y_scales", [P, Q], U8)
        out_rows = out_0.rearrange("(p j) q -> p j q", j=PACK)
        out_words = out_1[0].rearrange("p c r -> p (c r)").bitcast(I32)
        y_grouped = []
        for h in range(HALVES):
            w_codes, w_scales = w_quant[h]
            o = bank([P, PACK, P])
            for j in range(PACK):
                nc.tensor.matmul_mx(
                    out=o[:, j, :],
                    lhsT=v_codes[:, j * P : (j + 1) * P].bitcast(FP8X4),
                    lhsT_scale=v_scales[:, j * P : (j + 1) * P],
                    rhs=w_codes[:].bitcast(FP8X4),
                    rhs_scale=w_scales[:],
                    start=True,
                    stop=True,
                )
            fresh = sbuf("fresh%d" % h, [P, PACK, P], F32)
            nc.vector.tensor_tensor(
                out=fresh[:], in0=o[:], in1=let_go[:, h : h + 1, :].to_broadcast([P, PACK, P]), op=ALU.mult
            )
            y = sbuf("y%d" % h, [P, PACK, P], F32)
            nc.vector.tensor_tensor(out=y[:], in0=kept[h][:], in1=fresh[:], op=ALU.add)
            nc.sync.dma_start(out=out_rows[:, :, h * P : (h + 1) * P], in_=y[:])
            grouped = sbuf("y_grouped%d" % h, [P, P, PACK], BF16)
            grouped_view = grouped[:].rearrange("p (c i) j -> p c j i", i=PACK)
            y_view = y[:].rearrange("p j (c i) -> p c j i", i=PACK)
            if h == 0:
                nc.scalar.copy(out=grouped_view, in_=y_view)
            else:
                nc.vector.tensor_copy(out=grouped_view, in_=y_view)
            y_grouped.append(grouped)
        for h in range(HALVES):
            nc.vector.quantize_mx(
                out=y_codes[:, h * P : (h + 1) * P].bitcast(FP8X4),
                scales=y_scales[:, h * P : (h + 1) * P],
                in_=y_grouped[h][:].rearrange("p q j -> p (q j)"),
            )
            queue = nc.sync if h % 2 else nc.scalar
            queue.dma_start(out=out_words[:, h * P : (h + 1) * P], in_=y_codes[:, h * P : (h + 1) * P].bitcast(I32))
        for quad in range(QUADRANTS):
            queue = nc.sync if quad % 2 else nc.scalar
            queue.dma_start(
                out=out_2[0, 4 * quad : 4 * quad + 4, :].bitcast(I32),
                in_=y_scales[32 * quad : 32 * quad + 4, :].bitcast(I32),
            )
